import numpy as np
import ml_dtypes


def mxq(x, axis, fmt="e4m3"):
    dtype, down = {"e4m3": (ml_dtypes.float8_e4m3fn, 7), "e5m2": (ml_dtypes.float8_e5m2, 14)}[fmt]
    v = np.moveaxis(np.asarray(x, np.float32).astype(ml_dtypes.bfloat16).astype(np.float64), axis, -1)
    blocks = v.reshape(v.shape[:-1] + (-1, 32))
    amax = np.abs(blocks).max(-1, keepdims=True)
    byte = np.maximum(np.where(amax > 0, np.frexp(amax)[1] - 1 + 127, 0) - down, 1)
    scale = np.exp2(byte - 127.0)
    codes = (blocks / scale).astype(np.float32).astype(dtype).astype(np.float64)
    return np.moveaxis((codes * scale).reshape(v.shape), -1, axis)


WIDE = False


def mx_kscale(k):
    if not WIDE:
        return np.ones(k)
    levels = np.array([10, -10, 5, -5, 0])
    if k % 512:
        return np.exp2(np.random.permutation(np.resize(levels, k // 32))).repeat(32)
    a = np.empty((k // 512, 16))
    for p in range(k // 512):
        a[p, :8] = np.random.permutation(np.resize(levels, 8))
        for g in range(8):
            far = levels[np.abs(levels - a[p, g]) >= 10]
            a[p, g + 8] = far[np.random.randint(len(far))]
    return np.exp2(a.ravel()).repeat(32)


def f64(x):
    return np.asarray(x).astype(np.float64)


def striped(idx):
    return np.tile(idx.reshape(-1, 16).T, (8, 1)).astype(np.uint16)


def unstriped(offs):
    return offs[:16].T.reshape(-1).astype(np.int64)


def striped8(idx):
    return np.concatenate([x.reshape(-1, 16).T for x in idx]).astype(np.uint16)


def runs(offs, k):
    lists = np.stack([offs[16 * r : 16 * r + 16].T.reshape(-1) for r in range(8)]).astype(np.int64)
    return lists[np.arange(k) % 512 // 64]


def pack_weight(w):
    k, n = w.shape
    w = f64(np.asarray(w, np.float32).astype(ml_dtypes.bfloat16)).reshape(k // 32, 32, n)
    amax = np.abs(w).max(1)
    byte = np.clip(np.where(amax > 0, np.frexp(amax)[1] - 1 + 127 - 7, 1), 1, 254)
    scaled = (w * np.exp2(127.0 - byte)[:, None, :]).reshape(k, n).astype(np.float32)
    words = np.ascontiguousarray(scaled.reshape(k // 512, 128, 4, n).transpose(0, 1, 3, 2)).astype(ml_dtypes.float8_e4m3fn).view(np.uint8)
    return words, np.ascontiguousarray(byte.astype(np.uint8).reshape(k // 512, 16, n))


def unpack_weight(words, scales):
    g, p, n, _ = words.shape
    vals = np.ascontiguousarray(words).view(ml_dtypes.float8_e4m3fn).astype(np.float64) * np.repeat(np.exp2(scales.astype(np.float64) - 127.0), 8, axis=1)[..., None]
    return vals.transpose(0, 1, 3, 2).reshape(g * 512, n)


def sigmoid(v):
    return 1.0 / (1.0 + np.exp(-np.maximum(v, -700.0)))

def planes(y):
    n, m = y.shape
    v = y.astype(np.float32).astype(ml_dtypes.bfloat16).astype(np.float64).reshape(n // 32, 32, m)
    top = np.abs(v).max(1)
    byte = np.clip(np.where(top > 0, np.frexp(top)[1] - 1 + 127 - 7, 1), 1, 254)
    codes = (v * np.exp2(127.0 - byte)[:, None, :]).reshape(n, m).astype(np.float32).astype(ml_dtypes.float8_e4m3fn).view(np.uint8)
    words = codes.reshape(n // 512, 128, 4, m).transpose(0, 1, 3, 2)
    return np.ascontiguousarray(words), np.ascontiguousarray(byte.astype(np.uint8).reshape(n // 512, 16, m))


K, T, S, N, H = 512, 2048, 512, 512, 512


def setup_inputs():
    n = np.random.standard_normal
    s = mx_kscale(K)[:, None]
    u = mx_kscale(H)
    packed_xT = pack_weight(n((K, T)) * s)
    packed_w1 = pack_weight(n((K, H)) / np.sqrt(K) / s)
    packed_w2 = pack_weight(n((K, H)) / np.sqrt(K) / s)
    packed_w3 = pack_weight(n((H, N)) / np.sqrt(H) / u[:, None])
    return {
        "x_words": packed_xT[0],
        "x_scales": packed_xT[1],
        "w1_words": packed_w1[0],
        "w1_scales": packed_w1[1],
        "w2_words": packed_w2[0],
        "w2_scales": packed_w2[1],
        "gn": (np.random.uniform(0.5, 1.5, (H, 1)) * u[:, None]).astype(np.float32),
        "w3_words": packed_w3[0],
        "w3_scales": packed_w3[1],
        "offs": striped(np.random.permutation(T)[:S]),
        "two": striped(np.random.permutation(T)[:S]),
        "n1": striped8(np.stack([np.random.permutation(S) for _ in range(8)])),
        "n2": striped8(np.stack([np.random.permutation(S) for _ in range(8)])),
        "n3": striped8(np.stack([np.random.permutation(S) for _ in range(8)])),
        "n4": striped8(np.stack([np.random.permutation(S) for _ in range(8)])),
    }


def reference(x_words, x_scales, w1_words, w1_scales, w2_words, w2_scales, gn, w3_words, w3_scales, offs, two, n1, n2, n3, n4):
    xq = unpack_weight(x_words, x_scales)[:, unstriped(offs)]
    y = unpack_weight(w1_words, w1_scales).T @ xq
    x_two = unpack_weight(x_words, x_scales)[:, unstriped(two)]
    d = unpack_weight(w2_words, w2_scales).T @ x_two
    z = f64(gn) * (0.75 * (y * (d[np.arange(H)[:, None], runs(n2, H)]) - ((y[np.arange(H)[:, None], runs(n1, H)]) * d)))
    h = unpack_weight(w3_words, w3_scales).T @ mxq(z, 0, "e4m3")
    st = h[np.arange(N)[:, None], runs(n3, N)] - h
    out_0 = h * (sigmoid(st[np.arange(N)[:, None], runs(n4, N)]))
    return (out_0,) + planes(out_0)

@@ -1,0 +1,192 @@
+from contextlib import ExitStack
+
+import concourse.mybir as mybir
+
+K, T, S, H, N = 512, 2048, 512, 512, 512
+FLOPS = 3 * 2 * 512 * 512 * 512
+
+F32 = mybir.dt.float32
+BF16 = mybir.dt.bfloat16
+I32 = mybir.dt.int32
+U32 = mybir.dt.uint32
+U16 = mybir.dt.uint16
+U8 = mybir.dt.uint8
+FP8X4 = mybir.dt.float8_e4m3fn_x4
+MULT = mybir.AluOpType.mult
+SUBTRACT = mybir.AluOpType.subtract
+COPY = mybir.ActivationFunctionType.Copy
+SIGMOID = mybir.ActivationFunctionType.Sigmoid
+
+P = 128
+PACK = 4
+QUADRANTS = 4
+HALF = S // 2
+WINDOW = 2 * S
+
+
+def words_in_hbm(words):
+    return words[0].rearrange("p n t -> p (n t)").bitcast(I32)
+
+
+def load_scale_rows(queue, plane, first_row, scales):
+    for q in range(QUADRANTS):
+        rows = slice(32 * q + first_row, 32 * q + first_row + 4)
+        queue.dma_start(plane[rows, :].bitcast(I32), scales[0, 4 * q : 4 * q + 4, :].bitcast(I32))
+
+
+def deal_columns(nc, dealt, plain, run):
+    nc.vector.tensor_copy(
+        dealt[:].rearrange("p (t b i) -> p b t i", t=PACK, i=run),
+        plain[:].rearrange("p (b i t) -> p b t i", t=PACK, i=run),
+    )
+
+
+def by_rows(planes, cols):
+    return planes[:, :, cols].rearrange("p t (c i) -> p c t i", i=4)
+
+
+def woven(tile, cols):
+    return tile[:, PACK * cols.start : PACK * cols.stop].rearrange("p (c i t) -> p c t i", i=4, t=PACK)
+
+
+def tile_picked_twlcrossbhopd_none_po_kernel(
+    tc, x_words, x_scales, w1_words, w1_scales, w2_words, w2_scales, gn, w3_words, w3_scales,
+    offs, two, n1, n2, n3, n4, out_0, out_1, out_2,
+):
+    nc = tc.nc
+    halves = [slice(0, HALF), slice(HALF, S)]
+
+    with ExitStack() as ctx:
+        keep = ctx.enter_context(tc.tile_pool(name="keep", bufs=1))
+        psum = ctx.enter_context(tc.psum_pool(name="psum", bufs=1))
+
+        def sbuf(name, shape, dtype):
+            return keep.tile(shape, dtype, name=name, align_bytes=64)
+
+        def bank(index, width):
+            return psum.tile([P, width], F32, name="bank%d" % index)
+
+        lists = {name: sbuf("list_" + name, [P, S // 16], U16) for name in ("offs", "two", "n1", "n2", "n3", "n4")}
+        xw = sbuf("xw", [P, T], I32)
+        xs = sbuf("xs", [P, T], U8)
+        w_plain = [sbuf("w_plain%d" % i, [P, H], I32) for i in range(3)]
+        w_dealt = [sbuf("w_dealt%d" % i, [P, H], I32) for i in range(3)]
+        s12_plain = sbuf("s12_plain", [P, H], U8)
+        s12_dealt = sbuf("s12_dealt", [P, H], U8)
+        s3_plain = sbuf("s3_plain", [P, N], U8)
+        s3_dealt = sbuf("s3_dealt", [P, N], U8)
+        gain_in = sbuf("gain_in", [P, PACK], F32)
+        gain = sbuf("gain", [P, PACK], F32)
+        first = [sbuf("first%d" % t, [P, WINDOW], F32) for t in range(PACK)]
+        second = [sbuf("second%d" % t, [P, WINDOW], F32) for t in range(PACK)]
+
+        nc.gpsimd.memset(s12_plain[:].bitcast(I32), 0)
+        nc.gpsimd.memset(s3_plain[:].bitcast(I32), 0)
+        nc.sync.dma_start(lists["offs"][:], offs)
+        nc.sync.dma_start(lists["two"][:], two)
+        for q in range(QUADRANTS):
+            rows = x_scales[0, 4 * q : 4 * q + 4, :].bitcast(I32)
+            nc.scalar.dma_start(xs[32 * q : 32 * (q + 1), :].bitcast(I32), rows.unsqueeze(0).to_broadcast([8, 4, T // 4]))
+        nc.sync.dma_start(xw[:], words_in_hbm(x_words))
+        nc.sync.dma_start(w_plain[0][:], words_in_hbm(w1_words))
+        load_scale_rows(nc.gpsimd, s12_plain, 0, w1_scales)
+        load_scale_rows(nc.scalar, s12_plain, 4, w2_scales)
+        nc.sync.dma_start(w_plain[1][:], words_in_hbm(w2_words))
+        nc.sync.dma_start(gain_in[:], gn.rearrange("(p t) o -> p (t o)", t=PACK))
+        nc.sync.dma_start(lists["n2"][:], n2)
+        nc.sync.dma_start(lists["n1"][:], n1)
+        nc.sync.dma_start(w_plain[2][:], words_in_hbm(w3_words))
+        load_scale_rows(nc.gpsimd, s3_plain, 0, w3_scales)
+        nc.sync.dma_start(lists["n3"][:], n3)
+        nc.sync.dma_start(lists["n4"][:], n4)
+        nc.scalar.mul(gain[:], gain_in[:], 0.75)
+
+        picked_words = {name: sbuf("words_" + name, [P, S], U32) for name in ("offs", "two")}
+        picked_scales = {name: sbuf("scales_" + name, [P, S], U8) for name in ("offs", "two")}
+        for name in ("offs", "two"):
+            nc.vector.tensor_copy(picked_scales[name][:], xs[:].indirect(lists[name][:]))
+        nc.vector.tensor_copy(picked_words["offs"][:], xw[:].bitcast(U32).indirect(lists["offs"][:]))
+        deal_columns(nc, w_dealt[0], w_plain[0], 4)
+        deal_columns(nc, s12_dealt, s12_plain, 16)
+        nc.vector.tensor_copy(picked_words["two"][:], xw[:].bitcast(U32).indirect(lists["two"][:]))
+        deal_columns(nc, w_dealt[1], w_plain[1], 4)
+
+        def product(out, weights, plane, t, codes, scales):
+            cols = slice(P * t, P * (t + 1))
+            nc.tensor.matmul_mx(
+                out=out,
+                lhsT=weights[:, cols].bitcast(FP8X4),
+                lhsT_scale=plane[:, cols],
+                rhs=codes.bitcast(FP8X4),
+                rhs_scale=scales,
+                start=True,
+                stop=True,
+            )
+
+        for t in range(PACK):
+            acc = bank(t, S)
+            product(acc[:], w_dealt[0], s12_dealt[0:P, :], t, picked_words["offs"][:], picked_scales["offs"][:])
+            nc.scalar.activation(first[t][:, :S], acc[:], COPY, scale=gain[:, t : t + 1])
+        for t in range(PACK):
+            acc = bank(PACK + t, S)
+            product(acc[:], w_dealt[1], s12_dealt[4:P, :], t, picked_words["two"][:], picked_scales["two"][:])
+            nc.scalar.copy(second[t][:, :S], acc[:])
+
+        deal_columns(nc, w_dealt[2], w_plain[2], 4)
+        deal_columns(nc, s3_dealt, s3_plain, 16)
+
+        plus = sbuf("plus", [P, PACK, S], F32)
+        minus = sbuf("minus", [P, PACK, S], F32)
+        for t in range(PACK):
+            nc.vector.tensor_tensor(plus[:, t, :], second[t][:].indirect(lists["n2"][:]), first[t][:, :S], MULT)
+            nc.vector.tensor_tensor(minus[:, t, :], first[t][:].indirect(lists["n1"][:]), second[t][:, :S], MULT)
+
+        z = sbuf("z", [P, PACK * S], BF16)
+        z_words = sbuf("z_words", [P, S], U32)
+        z_scales = sbuf("z_scales", [P, S], U8)
+        for cols in halves:
+            nc.vector.tensor_tensor(woven(z, cols), by_rows(plus, cols), by_rows(minus, cols), SUBTRACT)
+        for cols in halves:
+            nc.vector.quantize_mx(
+                out=z_words[:, cols].bitcast(FP8X4),
+                scales=z_scales[:, cols],
+                in_=z[:, PACK * cols.start : PACK * cols.stop],
+            )
+
+        h = sbuf("h", [P, PACK, S], F32)
+        for c, cols in enumerate(halves):
+            acc = bank(PACK + c, HALF)
+            product(acc[:], w_dealt[2], s3_dealt[0:P, :], 0, z_words[:, cols], z_scales[:, cols])
+            nc.scalar.copy(second[0][:, cols], acc[:])
+            nc.vector.tensor_copy(h[:, 0, cols], second[0][:, cols])
+        for t in range(1, PACK):
+            acc = bank(t, S)
+            product(acc[:], w_dealt[2], s3_dealt[0:P, :], t, z_words[:], z_scales[:])
+            nc.scalar.copy(second[t][:, :S], acc[:])
+            nc.scalar.copy(h[:, t, :], acc[:])
+
+        gate = sbuf("gate", [P, PACK, S], F32)
+        result = sbuf("result", [P, PACK, S], F32)
+        out_rows = out_0.rearrange("(p t) s -> p t s", t=PACK)
+        for t in range(PACK):
+            nc.vector.tensor_tensor(first[t][:, :S], second[t][:].indirect(lists["n3"][:]), h[:, t, :], SUBTRACT)
+            nc.scalar.activation(gate[:, t, :], first[t][:].indirect(lists["n4"][:]), SIGMOID)
+        for t in range(PACK):
+            nc.vector.tensor_tensor(result[:, t, :], h[:, t, :], gate[:, t, :], MULT)
+            nc.sync.dma_start(out_rows[:, t, :], result[:, t, :])
+
+        rounded = sbuf("rounded", [P, PACK * S], BF16)
+        out_words = sbuf("out_words", [P, S], I32)
+        out_scales = sbuf("out_scales", [P, S], U8)
+        nc.vector.tensor_copy(woven(rounded, halves[0]), by_rows(result, halves[0]))
+        nc.scalar.copy(woven(rounded, halves[1]), by_rows(result, halves[1]))
+        for cols in halves:
+            nc.vector.quantize_mx(
+                out=out_words[:, cols].bitcast(FP8X4),
+                scales=out_scales[:, cols],
+                in_=rounded[:, PACK * cols.start : PACK * cols.stop],
+            )
+            nc.sync.dma_start(words_in_hbm(out_1)[:, cols], out_words[:, cols])
+        for q in range(QUADRANTS):
+            queue = nc.scalar if q % 2 else nc.sync
+            queue.dma_start(out_2[0, 4 * q : 4 * q + 4, :].bitcast(I32), out_scales[32 * q : 32 * q + 4, :].bitcast(I32))

@@ -28,16 +28,16 @@ def words_in_hbm(words):
     return words[0].rearrange("p n t -> p (n t)").bitcast(I32)
 
 
-def load_scale_rows(queue, plane, first_row, scales):
-    for q in range(QUADRANTS):
+def load_scale_rows(queues, plane, first_row, scales):
+    for q, queue in enumerate(queues):
         rows = slice(32 * q + first_row, 32 * q + first_row + 4)
         queue.dma_start(plane[rows, :].bitcast(I32), scales[0, 4 * q : 4 * q + 4, :].bitcast(I32))
 
 
-def deal_columns(nc, dealt, plain, run):
+def deal_columns(nc, dealt, plain, run, tiles=slice(0, PACK)):
     nc.vector.tensor_copy(
-        dealt[:].rearrange("p (t b i) -> p b t i", t=PACK, i=run),
-        plain[:].rearrange("p (b i t) -> p b t i", t=PACK, i=run),
+        dealt[:].rearrange("p (t b i) -> p b t i", t=PACK, i=run)[:, :, tiles, :],
+        plain[:].rearrange("p (b i t) -> p b t i", t=PACK, i=run)[:, :, tiles, :],
     )
 
 
@@ -69,47 +69,53 @@ def tile_picked_twlcrossbhopd_none_po_kernel(
         lists = {name: sbuf("list_" + name, [P, S // 16], U16) for name in ("offs", "two", "n1", "n2", "n3", "n4")}
         xw = sbuf("xw", [P, T], I32)
         xs = sbuf("xs", [P, T], U8)
-        w_plain = [sbuf("w_plain%d" % i, [P, H], I32) for i in range(3)]
+        w_plain = [sbuf("w_plain%d" % i, [P, H], I32) for i in range(2)]
+        w_plain.append(keep.tile([P, H], I32, name="w3_plain", tag="shared", align_bytes=64))
         w_dealt = [sbuf("w_dealt%d" % i, [P, H], I32) for i in range(3)]
-        s12_plain = sbuf("s12_plain", [P, H], U8)
+        s12_plain = keep.tile([P, H], U8, name="s12_plain", tag="shared12", align_bytes=64)
         s12_dealt = sbuf("s12_dealt", [P, H], U8)
-        s3_plain = sbuf("s3_plain", [P, N], U8)
+        s3_plain = keep.tile([P, N], U8, name="s3_plain", tag="shared3", align_bytes=64)
         s3_dealt = sbuf("s3_dealt", [P, N], U8)
         gain_in = sbuf("gain_in", [P, PACK], F32)
         gain = sbuf("gain", [P, PACK], F32)
         first = [sbuf("first%d" % t, [P, WINDOW], F32) for t in range(PACK)]
         second = [sbuf("second%d" % t, [P, WINDOW], F32) for t in range(PACK)]
 
-        nc.gpsimd.memset(s12_plain[:].bitcast(I32), 0)
-        nc.gpsimd.memset(s3_plain[:].bitcast(I32), 0)
+        warm = sbuf("warm", [P, 2], F32)
+        nc.gpsimd.memset(xs[:].bitcast(I32), 0)
+        nc.vector.memset(s12_plain[:].bitcast(I32), 0)
+        nc.vector.memset(warm[:, 0:1], 0.0)
+        nc.vector.memset(s3_plain[:].bitcast(I32), 0)
+        nc.scalar.activation(warm[:, 1:2], warm[:, 0:1], SIGMOID)
         nc.sync.dma_start(lists["offs"][:], offs)
         nc.sync.dma_start(lists["two"][:], two)
-        for q in range(QUADRANTS):
-            rows = x_scales[0, 4 * q : 4 * q + 4, :].bitcast(I32)
-            nc.scalar.dma_start(xs[32 * q : 32 * (q + 1), :].bitcast(I32), rows.unsqueeze(0).to_broadcast([8, 4, T // 4]))
+        load_scale_rows([nc.sync] * 4, xs, 0, x_scales)
         nc.sync.dma_start(xw[:], words_in_hbm(x_words))
         nc.sync.dma_start(w_plain[0][:], words_in_hbm(w1_words))
-        load_scale_rows(nc.gpsimd, s12_plain, 0, w1_scales)
-        load_scale_rows(nc.scalar, s12_plain, 4, w2_scales)
         nc.sync.dma_start(w_plain[1][:], words_in_hbm(w2_words))
+        load_scale_rows([nc.sync] * 4, s12_plain, 0, w1_scales)
+        load_scale_rows([nc.gpsimd] * 3 + [nc.sync], s12_plain, 4, w2_scales)
         nc.sync.dma_start(gain_in[:], gn.rearrange("(p t) o -> p (t o)", t=PACK))
         nc.sync.dma_start(lists["n2"][:], n2)
         nc.sync.dma_start(lists["n1"][:], n1)
+        load_scale_rows([nc.sync] * 4, s3_plain, 0, w3_scales)
         nc.sync.dma_start(w_plain[2][:], words_in_hbm(w3_words))
-        load_scale_rows(nc.gpsimd, s3_plain, 0, w3_scales)
         nc.sync.dma_start(lists["n3"][:], n3)
         nc.sync.dma_start(lists["n4"][:], n4)
         nc.scalar.mul(gain[:], gain_in[:], 0.75)
 
-        picked_words = {name: sbuf("words_" + name, [P, S], U32) for name in ("offs", "two")}
+        picked_words = {"offs": sbuf("words_offs", [P, S], U32)}
         picked_scales = {name: sbuf("scales_" + name, [P, S], U8) for name in ("offs", "two")}
         for name in ("offs", "two"):
             nc.vector.tensor_copy(picked_scales[name][:], xs[:].indirect(lists[name][:]))
         nc.vector.tensor_copy(picked_words["offs"][:], xw[:].bitcast(U32).indirect(lists["offs"][:]))
-        deal_columns(nc, w_dealt[0], w_plain[0], 4)
         deal_columns(nc, s12_dealt, s12_plain, 16)
+        for i in range(2):
+            deal_columns(nc, w_dealt[i], w_plain[i], 4, slice(0, 1))
+        picked_words["two"] = keep.tile([P, S], U32, name="words_two", tag="shared12", align_bytes=64)
         nc.vector.tensor_copy(picked_words["two"][:], xw[:].bitcast(U32).indirect(lists["two"][:]))
-        deal_columns(nc, w_dealt[1], w_plain[1], 4)
+        for i in range(2):
+            deal_columns(nc, w_dealt[i], w_plain[i], 4, slice(1, PACK))
 
         def product(out, weights, plane, t, codes, scales):
             cols = slice(P * t, P * (t + 1))
@@ -127,16 +133,15 @@ def tile_picked_twlcrossbhopd_none_po_kernel(
             acc = bank(t, S)
             product(acc[:], w_dealt[0], s12_dealt[0:P, :], t, picked_words["offs"][:], picked_scales["offs"][:])
             nc.scalar.activation(first[t][:, :S], acc[:], COPY, scale=gain[:, t : t + 1])
-        for t in range(PACK):
             acc = bank(PACK + t, S)
             product(acc[:], w_dealt[1], s12_dealt[4:P, :], t, picked_words["two"][:], picked_scales["two"][:])
             nc.scalar.copy(second[t][:, :S], acc[:])
 
-        deal_columns(nc, w_dealt[2], w_plain[2], 4)
         deal_columns(nc, s3_dealt, s3_plain, 16)
+        deal_columns(nc, w_dealt[2], w_plain[2], 4)
 
-        plus = sbuf("plus", [P, PACK, S], F32)
-        minus = sbuf("minus", [P, PACK, S], F32)
+        plus = keep.tile([P, PACK, S], F32, name="plus", tag="shared", align_bytes=64)
+        minus = keep.tile([P, PACK, S], F32, name="minus", tag="shared3", align_bytes=64)
         for t in range(PACK):
             nc.vector.tensor_tensor(plus[:, t, :], second[t][:].indirect(lists["n2"][:]), first[t][:, :S], MULT)
             nc.vector.tensor_tensor(minus[:, t, :], first[t][:].indirect(lists["n1"][:]), second[t][:, :S], MULT)
@@ -163,23 +168,39 @@ def tile_picked_twlcrossbhopd_none_po_kernel(
             acc = bank(t, S)
             product(acc[:], w_dealt[2], s3_dealt[0:P, :], t, z_words[:], z_scales[:])
             nc.scalar.copy(second[t][:, :S], acc[:])
-            nc.scalar.copy(h[:, t, :], acc[:])
 
         gate = sbuf("gate", [P, PACK, S], F32)
         result = sbuf("result", [P, PACK, S], F32)
         out_rows = out_0.rearrange("(p t) s -> p t s", t=PACK)
-        for t in range(PACK):
+        last = PACK - 1
+
+        def difference(t):
+            if t:
+                nc.vector.tensor_copy(h[:, t, :], second[t][:, :S])
             nc.vector.tensor_tensor(first[t][:, :S], second[t][:].indirect(lists["n3"][:]), h[:, t, :], SUBTRACT)
+
+        def finish(t, cols, factor):
+            nc.vector.tensor_tensor(result[:, t, cols], h[:, t, cols], factor, MULT)
+            nc.sync.dma_start(out_rows[:, t, cols], result[:, t, cols])
+
+        for t in range(last):
+            difference(t)
             nc.scalar.activation(gate[:, t, :], first[t][:].indirect(lists["n4"][:]), SIGMOID)
-        for t in range(PACK):
-            nc.vector.tensor_tensor(result[:, t, :], h[:, t, :], gate[:, t, :], MULT)
-            nc.sync.dma_start(out_rows[:, t, :], result[:, t, :])
+        difference(last)
+        for cols in halves:
+            entries = lists["n4"][:, cols.start // 16 : cols.stop // 16]
+            nc.scalar.activation(gate[:, last, cols], first[last][:].indirect(entries), SIGMOID)
+        for t in range(last):
+            finish(t, slice(0, S), gate[:, t, :])
 
         rounded = sbuf("rounded", [P, PACK * S], BF16)
         out_words = sbuf("out_words", [P, S], I32)
         out_scales = sbuf("out_scales", [P, S], U8)
+        finish(last, halves[0], gate[:, last, halves[0]])
         nc.vector.tensor_copy(woven(rounded, halves[0]), by_rows(result, halves[0]))
-        nc.scalar.copy(woven(rounded, halves[1]), by_rows(result, halves[1]))
+        finish(last, halves[1], gate[:, last, halves[1]])
+        nc.scalar.copy(woven(rounded, slice(256, 384)), by_rows(result, slice(256, 384)))
+        nc.vector.tensor_copy(woven(rounded, slice(384, 512)), by_rows(result, slice(384, 512)))
         for cols in halves:
             nc.vector.quantize_mx(
                 out=out_words[:, cols].bitcast(FP8X4),

@@ -88,8 +88,8 @@ def tile_picked_twlcrossbhopd_none_po_kernel(
         nc.vector.memset(s3_plain[:].bitcast(I32), 0)
         nc.scalar.activation(warm[:, 1:2], warm[:, 0:1], SIGMOID)
         nc.sync.dma_start(lists["offs"][:], offs)
+        load_scale_rows([nc.sync, nc.scalar] * 2, xs, 0, x_scales)
         nc.sync.dma_start(lists["two"][:], two)
-        load_scale_rows([nc.sync] * 4, xs, 0, x_scales)
         nc.sync.dma_start(xw[:], words_in_hbm(x_words))
         nc.sync.dma_start(w_plain[0][:], words_in_hbm(w1_words))
         nc.sync.dma_start(w_plain[1][:], words_in_hbm(w2_words))
@@ -111,11 +111,11 @@ def tile_picked_twlcrossbhopd_none_po_kernel(
         nc.vector.tensor_copy(picked_words["offs"][:], xw[:].bitcast(U32).indirect(lists["offs"][:]))
         deal_columns(nc, s12_dealt, s12_plain, 16)
         for i in range(2):
-            deal_columns(nc, w_dealt[i], w_plain[i], 4, slice(0, 1))
+            nc.gpsimd.tensor_copy(
+                w_dealt[i][:].rearrange("p (t m) -> p t m", t=PACK), w_plain[i][:].rearrange("p (m t) -> p t m", t=PACK)
+            )
         picked_words["two"] = keep.tile([P, S], U32, name="words_two", tag="shared12", align_bytes=64)
         nc.vector.tensor_copy(picked_words["two"][:], xw[:].bitcast(U32).indirect(lists["two"][:]))
-        for i in range(2):
-            deal_columns(nc, w_dealt[i], w_plain[i], 4, slice(1, PACK))
 
         def product(out, weights, plane, t, codes, scales):
             cols = slice(P * t, P * (t + 1))
@@ -130,10 +130,10 @@ def tile_picked_twlcrossbhopd_none_po_kernel(
             )
 
         for t in range(PACK):
-            acc = bank(t, S)
+            acc = bank(t if t < 2 else PACK + t - 2, S)
             product(acc[:], w_dealt[0], s12_dealt[0:P, :], t, picked_words["offs"][:], picked_scales["offs"][:])
             nc.scalar.activation(first[t][:, :S], acc[:], COPY, scale=gain[:, t : t + 1])
-            acc = bank(PACK + t, S)
+            acc = bank(PACK + t if t < 2 else t, S)
             product(acc[:], w_dealt[1], s12_dealt[4:P, :], t, picked_words["two"][:], picked_scales["two"][:])
             nc.scalar.copy(second[t][:, :S], acc[:])
 
@@ -149,25 +149,30 @@ def tile_picked_twlcrossbhopd_none_po_kernel(
         z = sbuf("z", [P, PACK * S], BF16)
         z_words = sbuf("z_words", [P, S], U32)
         z_scales = sbuf("z_scales", [P, S], U8)
-        for cols in halves:
-            nc.vector.tensor_tensor(woven(z, cols), by_rows(plus, cols), by_rows(minus, cols), SUBTRACT)
-        for cols in halves:
-            nc.vector.quantize_mx(
-                out=z_words[:, cols].bitcast(FP8X4),
-                scales=z_scales[:, cols],
-                in_=z[:, PACK * cols.start : PACK * cols.stop],
-            )
+        pieces = [slice(0, 256), slice(256, 384), slice(384, 512)]
+        for ahead, cols in zip(pieces + [None], [None] + pieces):
+            if ahead:
+                nc.vector.tensor_tensor(woven(z, ahead), by_rows(plus, ahead), by_rows(minus, ahead), SUBTRACT)
+            if cols:
+                nc.vector.quantize_mx(
+                    out=z_words[:, cols].bitcast(FP8X4),
+                    scales=z_scales[:, cols],
+                    in_=z[:, PACK * cols.start : PACK * cols.stop],
+                )
 
         h = sbuf("h", [P, PACK, S], F32)
-        for c, cols in enumerate(halves):
-            acc = bank(PACK + c, HALF)
+        for c, cols in enumerate(pieces):
+            acc = bank(PACK + c, cols.stop - cols.start)
             product(acc[:], w_dealt[2], s3_dealt[0:P, :], 0, z_words[:, cols], z_scales[:, cols])
             nc.scalar.copy(second[0][:, cols], acc[:])
             nc.vector.tensor_copy(h[:, 0, cols], second[0][:, cols])
-        for t in range(1, PACK):
-            acc = bank(t, S)
-            product(acc[:], w_dealt[2], s3_dealt[0:P, :], t, z_words[:], z_scales[:])
-            nc.scalar.copy(second[t][:, :S], acc[:])
+        for c, cols in enumerate(halves):
+            for t in range(1, PACK):
+                acc = bank((3 * c + t + 6) % 8, HALF)
+                product(acc[:], w_dealt[2], s3_dealt[0:P, :], t, z_words[:, cols], z_scales[:, cols])
+                nc.scalar.copy(second[t][:, cols], acc[:])
+        for t in range(2, PACK):
+            nc.scalar.copy(h[:, t, halves[1]], second[t][:, halves[1]])
 
         gate = sbuf("gate", [P, PACK, S], F32)
         result = sbuf("result", [P, PACK, S], F32)
@@ -175,8 +180,8 @@ def tile_picked_twlcrossbhopd_none_po_kernel(
         last = PACK - 1
 
         def difference(t):
-            if t:
-                nc.vector.tensor_copy(h[:, t, :], second[t][:, :S])
+            if t == 1:
+                nc.vector.tensor_copy(h[:, t, halves[1]], second[t][:, halves[1]])
             nc.vector.tensor_tensor(first[t][:, :S], second[t][:].indirect(lists["n3"][:]), h[:, t, :], SUBTRACT)
 
         def finish(t, cols, factor):
@@ -185,6 +190,9 @@ def tile_picked_twlcrossbhopd_none_po_kernel(
 
         for t in range(last):
             difference(t)
+            if t == 0:
+                for later in range(1, PACK):
+                    nc.vector.tensor_copy(h[:, later, halves[0]], second[later][:, halves[0]])
             nc.scalar.activation(gate[:, t, :], first[t][:].indirect(lists["n4"][:]), SIGMOID)
         difference(last)
         for cols in halves:

@@ -3,7 +3,7 @@ from contextlib import ExitStack
 import concourse.mybir as mybir
 
 K, T, S, H, N = 512, 2048, 512, 512, 512
-FLOPS = 3 * 2 * 512 * 512 * 512
+FLOPS = 2 * S * (2 * K * H + H * N)
 
 F32 = mybir.dt.float32
 BF16 = mybir.dt.bfloat16
@@ -19,34 +19,66 @@ SIGMOID = mybir.ActivationFunctionType.Sigmoid
 
 P = 128
 PACK = 4
-QUADRANTS = 4
+QUADRANT = 32
+QUADRANTS = P // QUADRANT
+SCALE_ROWS = 4
+GROUP = 16
+BANKS = 8
 HALF = S // 2
 WINDOW = 2 * S
+WORD_RUN, BYTE_RUN = 4, 16
 
 
 def words_in_hbm(words):
     return words[0].rearrange("p n t -> p (n t)").bitcast(I32)
 
 
-def load_scale_rows(queues, plane, first_row, scales):
+def scale_partitions(q, first):
+    return slice(QUADRANT * q + first, QUADRANT * q + first + SCALE_ROWS)
+
+
+def scale_rows_in_hbm(scales, q):
+    return scales[0, SCALE_ROWS * q : SCALE_ROWS * (q + 1), :].bitcast(I32)
+
+
+def load_scale_rows(queues, plane, first, scales):
     for q, queue in enumerate(queues):
-        rows = slice(32 * q + first_row, 32 * q + first_row + 4)
-        queue.dma_start(plane[rows, :].bitcast(I32), scales[0, 4 * q : 4 * q + 4, :].bitcast(I32))
+        queue.dma_start(plane[scale_partitions(q, first), :].bitcast(I32), scale_rows_in_hbm(scales, q))
 
 
-def deal_columns(nc, dealt, plain, run, tiles=slice(0, PACK)):
+def deal_columns(nc, dealt, plain, run):
     nc.vector.tensor_copy(
-        dealt[:].rearrange("p (t b i) -> p b t i", t=PACK, i=run)[:, :, tiles, :],
-        plain[:].rearrange("p (b i t) -> p b t i", t=PACK, i=run)[:, :, tiles, :],
+        dealt[:].rearrange("p (t b i) -> p b t i", t=PACK, i=run),
+        plain[:].rearrange("p (b i t) -> p b t i", t=PACK, i=run),
     )
 
 
-def by_rows(planes, cols):
-    return planes[:, :, cols].rearrange("p t (c i) -> p c t i", i=4)
+def by_runs(tiles, cols):
+    return tiles[:, :, cols].rearrange("p t (c i) -> p c t i", i=WORD_RUN)
 
 
 def woven(tile, cols):
-    return tile[:, PACK * cols.start : PACK * cols.stop].rearrange("p (c i t) -> p c t i", i=4, t=PACK)
+    return tile[:, PACK * cols.start : PACK * cols.stop].rearrange("p (c i t) -> p c t i", i=WORD_RUN, t=PACK)
+
+
+def quantise(nc, words, scales, values, cols):
+    nc.vector.quantize_mx(
+        out=words[:, cols].bitcast(FP8X4),
+        scales=scales[:, cols],
+        in_=values[:, PACK * cols.start : PACK * cols.stop],
+    )
+
+
+def product(nc, out, weights, plane, t, codes, scales):
+    nc.tensor.matmul_mx(
+        out=out,
+        lhsT=weights.bitcast(FP8X4),
+        lhsT_scale=plane[:, P * t : P * (t + 1)],
+        rhs=codes.bitcast(FP8X4),
+        rhs_scale=scales,
+        start=True,
+        stop=True,
+    )
 
 
 def tile_picked_twlcrossbhopd_none_po_kernel(
@@ -55,31 +87,33 @@ def tile_picked_twlcrossbhopd_none_po_kernel(
 ):
     nc = tc.nc
     halves = [slice(0, HALF), slice(HALF, S)]
+    last = PACK - 1
 
     with ExitStack() as ctx:
         keep = ctx.enter_context(tc.tile_pool(name="keep", bufs=1))
         psum = ctx.enter_context(tc.psum_pool(name="psum", bufs=1))
 
-        def sbuf(name, shape, dtype):
-            return keep.tile(shape, dtype, name=name, align_bytes=64)
+        def sbuf(name, shape, dtype, slot=""):
+            return keep.tile(shape, dtype, name=name, tag=slot, align_bytes=64)
 
         def bank(index, width):
             return psum.tile([P, width], F32, name="bank%d" % index)
 
-        lists = {name: sbuf("list_" + name, [P, S // 16], U16) for name in ("offs", "two", "n1", "n2", "n3", "n4")}
-        xw = sbuf("xw", [P, T], I32)
+        lists = {name: sbuf("list_" + name, [P, S // GROUP], U16) for name in ("offs", "two", "n1", "n2", "n3", "n4")}
+        xw = sbuf("xw", [P, T], I32, slot="x_words_slot")
         xs = sbuf("xs", [P, T], U8)
-        w_plain = [sbuf("w_plain%d" % i, [P, H], I32) for i in range(2)]
-        w_plain.append(keep.tile([P, H], I32, name="w3_plain", tag="shared", align_bytes=64))
-        w_dealt = [sbuf("w_dealt%d" % i, [P, H], I32) for i in range(3)]
-        s12_plain = keep.tile([P, H], U8, name="s12_plain", tag="shared12", align_bytes=64)
-        s12_dealt = sbuf("s12_dealt", [P, H], U8)
-        s3_plain = keep.tile([P, N], U8, name="s3_plain", tag="shared3", align_bytes=64)
+        w12_plain = sbuf("w12_plain", [P, 2, H], I32)
+        w12_first = sbuf("w12_first", [P, 2, P], I32)
+        w3_plain = sbuf("w3_plain", [P, N], I32, slot="w3_words_slot")
+        w3_dealt = sbuf("w3_dealt", [P, N], I32)
         s3_dealt = sbuf("s3_dealt", [P, N], U8)
+        s12_plain = sbuf("s12_plain", [P, H], U8, slot="w12_scales_slot")
+        s12_dealt = sbuf("s12_dealt", [P, H], U8)
+        s3_plain = sbuf("s3_plain", [P, N], U8, slot="w3_scales_slot")
         gain_in = sbuf("gain_in", [P, PACK], F32)
         gain = sbuf("gain", [P, PACK], F32)
-        first = [sbuf("first%d" % t, [P, WINDOW], F32) for t in range(PACK)]
-        second = [sbuf("second%d" % t, [P, WINDOW], F32) for t in range(PACK)]
+        y_or_st = [sbuf("y_or_st%d" % t, [P, WINDOW], F32) for t in range(PACK)]
+        d_or_h = [sbuf("d_or_h%d" % t, [P, WINDOW], F32) for t in range(PACK)]
 
         warm = sbuf("warm", [P, 2], F32)
         nc.gpsimd.memset(xs[:].bitcast(I32), 0)
@@ -87,135 +121,129 @@ def tile_picked_twlcrossbhopd_none_po_kernel(
         nc.vector.memset(warm[:, 0:1], 0.0)
         nc.vector.memset(s3_plain[:].bitcast(I32), 0)
         nc.scalar.activation(warm[:, 1:2], warm[:, 0:1], SIGMOID)
+
         nc.sync.dma_start(lists["offs"][:], offs)
-        load_scale_rows([nc.sync, nc.scalar] * 2, xs, 0, x_scales)
         nc.sync.dma_start(lists["two"][:], two)
+        load_scale_rows([nc.sync] * QUADRANTS, xs, 0, x_scales)
         nc.sync.dma_start(xw[:], words_in_hbm(x_words))
-        nc.sync.dma_start(w_plain[0][:], words_in_hbm(w1_words))
-        nc.sync.dma_start(w_plain[1][:], words_in_hbm(w2_words))
-        load_scale_rows([nc.sync] * 4, s12_plain, 0, w1_scales)
-        load_scale_rows([nc.gpsimd] * 3 + [nc.sync], s12_plain, 4, w2_scales)
+        nc.sync.dma_start(w12_plain[:, 0, :], words_in_hbm(w1_words))
+        nc.sync.dma_start(w12_plain[:, 1, :], words_in_hbm(w2_words))
+        load_scale_rows([nc.sync] * QUADRANTS, s12_plain, 0, w1_scales)
+        load_scale_rows([nc.gpsimd, nc.gpsimd, nc.gpsimd, nc.sync], s12_plain, SCALE_ROWS, w2_scales)
         nc.sync.dma_start(gain_in[:], gn.rearrange("(p t) o -> p (t o)", t=PACK))
         nc.sync.dma_start(lists["n2"][:], n2)
         nc.sync.dma_start(lists["n1"][:], n1)
-        load_scale_rows([nc.sync] * 4, s3_plain, 0, w3_scales)
-        nc.sync.dma_start(w_plain[2][:], words_in_hbm(w3_words))
+        load_scale_rows([nc.sync] * QUADRANTS, s3_plain, 0, w3_scales)
+        nc.sync.dma_start(w3_plain[:], words_in_hbm(w3_words))
         nc.sync.dma_start(lists["n3"][:], n3)
         nc.sync.dma_start(lists["n4"][:], n4)
         nc.scalar.mul(gain[:], gain_in[:], 0.75)
 
-        picked_words = {"offs": sbuf("words_offs", [P, S], U32)}
-        picked_scales = {name: sbuf("scales_" + name, [P, S], U8) for name in ("offs", "two")}
-        for name in ("offs", "two"):
-            nc.vector.tensor_copy(picked_scales[name][:], xs[:].indirect(lists[name][:]))
-        nc.vector.tensor_copy(picked_words["offs"][:], xw[:].bitcast(U32).indirect(lists["offs"][:]))
-        deal_columns(nc, s12_dealt, s12_plain, 16)
-        for i in range(2):
-            nc.gpsimd.tensor_copy(
-                w_dealt[i][:].rearrange("p (t m) -> p t m", t=PACK), w_plain[i][:].rearrange("p (m t) -> p t m", t=PACK)
-            )
-        picked_words["two"] = keep.tile([P, S], U32, name="words_two", tag="shared12", align_bytes=64)
-        nc.vector.tensor_copy(picked_words["two"][:], xw[:].bitcast(U32).indirect(lists["two"][:]))
-
-        def product(out, weights, plane, t, codes, scales):
-            cols = slice(P * t, P * (t + 1))
-            nc.tensor.matmul_mx(
-                out=out,
-                lhsT=weights[:, cols].bitcast(FP8X4),
-                lhsT_scale=plane[:, cols],
-                rhs=codes.bitcast(FP8X4),
-                rhs_scale=scales,
-                start=True,
-                stop=True,
-            )
+        words_offs = sbuf("words_offs", [P, S], U32)
+        scales_offs = sbuf("scales_offs", [P, S], U8)
+        scales_two = sbuf("scales_two", [P, S], U8)
+        nc.vector.tensor_copy(scales_offs[:], xs[:].indirect(lists["offs"][:]))
+        nc.vector.tensor_copy(scales_two[:], xs[:].indirect(lists["two"][:]))
+        nc.vector.tensor_copy(words_offs[:], xw[:].bitcast(U32).indirect(lists["offs"][:]))
+        w12_by_tile = w12_plain[:].rearrange("p w (b i t) -> p w b t i", t=PACK, i=WORD_RUN)
+        nc.vector.tensor_copy(w12_first[:].rearrange("p w (b i) -> p w b i", i=WORD_RUN), w12_by_tile[:, :, :, 0, :])
+        deal_columns(nc, s12_dealt, s12_plain, BYTE_RUN)
+        words_two = sbuf("words_two", [P, S], U32, slot="w12_scales_slot")
+        nc.vector.tensor_copy(words_two[:], xw[:].bitcast(U32).indirect(lists["two"][:]))
+        w12_rest = sbuf("w12_rest", [P, 2, last, P], I32, slot="x_words_slot")
+        nc.vector.tensor_copy(
+            w12_rest[:].rearrange("p w t (b i) -> p w b t i", i=WORD_RUN), w12_by_tile[:, :, :, 1:, :]
+        )
 
         for t in range(PACK):
-            acc = bank(t if t < 2 else PACK + t - 2, S)
-            product(acc[:], w_dealt[0], s12_dealt[0:P, :], t, picked_words["offs"][:], picked_scales["offs"][:])
-            nc.scalar.activation(first[t][:, :S], acc[:], COPY, scale=gain[:, t : t + 1])
-            acc = bank(PACK + t if t < 2 else t, S)
-            product(acc[:], w_dealt[1], s12_dealt[4:P, :], t, picked_words["two"][:], picked_scales["two"][:])
-            nc.scalar.copy(second[t][:, :S], acc[:])
+            w12_tile = w12_rest[:, :, t - 1, :] if t else w12_first[:]
+            acc = bank(t, S)
+            product(nc, acc[:], w12_tile[:, 0, :], s12_dealt[0:P, :], t, words_offs[:], scales_offs[:])
+            nc.scalar.activation(y_or_st[t][:, :S], acc[:], COPY, scale=gain[:, t : t + 1])
+            acc = bank(PACK + t, S)
+            product(nc, acc[:], w12_tile[:, 1, :], s12_dealt[SCALE_ROWS:P, :], t, words_two[:], scales_two[:])
+            nc.scalar.copy(d_or_h[t][:, :S], acc[:])
 
-        deal_columns(nc, s3_dealt, s3_plain, 16)
-        deal_columns(nc, w_dealt[2], w_plain[2], 4)
+        deal_columns(nc, s3_dealt, s3_plain, BYTE_RUN)
+        deal_columns(nc, w3_dealt, w3_plain, WORD_RUN)
 
-        plus = keep.tile([P, PACK, S], F32, name="plus", tag="shared", align_bytes=64)
-        minus = keep.tile([P, PACK, S], F32, name="minus", tag="shared3", align_bytes=64)
+        plus = sbuf("plus", [P, PACK, S], F32, slot="w3_words_slot")
+        minus = sbuf("minus", [P, PACK, S], F32, slot="w3_scales_slot")
         for t in range(PACK):
-            nc.vector.tensor_tensor(plus[:, t, :], second[t][:].indirect(lists["n2"][:]), first[t][:, :S], MULT)
-            nc.vector.tensor_tensor(minus[:, t, :], first[t][:].indirect(lists["n1"][:]), second[t][:, :S], MULT)
+            nc.vector.tensor_tensor(plus[:, t, :], d_or_h[t][:].indirect(lists["n2"][:]), y_or_st[t][:, :S], MULT)
+            nc.vector.tensor_tensor(minus[:, t, :], y_or_st[t][:].indirect(lists["n1"][:]), d_or_h[t][:, :S], MULT)
 
         z = sbuf("z", [P, PACK * S], BF16)
         z_words = sbuf("z_words", [P, S], U32)
         z_scales = sbuf("z_scales", [P, S], U8)
-        pieces = [slice(0, 256), slice(256, 384), slice(384, 512)]
-        for ahead, cols in zip(pieces + [None], [None] + pieces):
-            if ahead:
-                nc.vector.tensor_tensor(woven(z, ahead), by_rows(plus, ahead), by_rows(minus, ahead), SUBTRACT)
-            if cols:
-                nc.vector.quantize_mx(
-                    out=z_words[:, cols].bitcast(FP8X4),
-                    scales=z_scales[:, cols],
-                    in_=z[:, PACK * cols.start : PACK * cols.stop],
-                )
+        quarters = [slice(HALF, HALF + S // 4), slice(HALF + S // 4, S)]
+        pieces = [halves[0]] + quarters
+        for c, cols in enumerate(pieces):
+            nc.vector.tensor_tensor(woven(z, cols), by_runs(plus, cols), by_runs(minus, cols), SUBTRACT)
+            if c:
+                quantise(nc, z_words, z_scales, z, pieces[c - 1])
+        quantise(nc, z_words, z_scales, z, pieces[-1])
 
-        h = sbuf("h", [P, PACK, S], F32)
+        h_plain = sbuf("h_plain", [P, PACK, S], F32)
         for c, cols in enumerate(pieces):
             acc = bank(PACK + c, cols.stop - cols.start)
-            product(acc[:], w_dealt[2], s3_dealt[0:P, :], 0, z_words[:, cols], z_scales[:, cols])
-            nc.scalar.copy(second[0][:, cols], acc[:])
-            nc.vector.tensor_copy(h[:, 0, cols], second[0][:, cols])
+            product(nc, acc[:], w3_dealt[:, :P], s3_dealt[:], 0, z_words[:, cols], z_scales[:, cols])
+            nc.scalar.copy(d_or_h[0][:, cols], acc[:])
+            nc.vector.tensor_copy(h_plain[:, 0, cols], d_or_h[0][:, cols])
+        next_bank = PACK + len(pieces)
         for c, cols in enumerate(halves):
             for t in range(1, PACK):
-                acc = bank((3 * c + t + 6) % 8, HALF)
-                product(acc[:], w_dealt[2], s3_dealt[0:P, :], t, z_words[:, cols], z_scales[:, cols])
-                nc.scalar.copy(second[t][:, cols], acc[:])
+                acc = bank((next_bank + last * c + t - 1) % BANKS, HALF)
+                product(
+                    nc, acc[:], w3_dealt[:, P * t : P * (t + 1)], s3_dealt[:], t, z_words[:, cols], z_scales[:, cols]
+                )
+                nc.scalar.copy(d_or_h[t][:, cols], acc[:])
         for t in range(2, PACK):
-            nc.scalar.copy(h[:, t, halves[1]], second[t][:, halves[1]])
+            nc.scalar.copy(h_plain[:, t, halves[1]], d_or_h[t][:, halves[1]])
 
         gate = sbuf("gate", [P, PACK, S], F32)
         result = sbuf("result", [P, PACK, S], F32)
         out_rows = out_0.rearrange("(p t) s -> p t s", t=PACK)
-        last = PACK - 1
 
-        def difference(t):
-            if t == 1:
-                nc.vector.tensor_copy(h[:, t, halves[1]], second[t][:, halves[1]])
-            nc.vector.tensor_tensor(first[t][:, :S], second[t][:].indirect(lists["n3"][:]), h[:, t, :], SUBTRACT)
+        def make_st(t):
+            nc.vector.tensor_tensor(
+                y_or_st[t][:, :S], d_or_h[t][:].indirect(lists["n3"][:]), h_plain[:, t, :], SUBTRACT
+            )
 
-        def finish(t, cols, factor):
-            nc.vector.tensor_tensor(result[:, t, cols], h[:, t, cols], factor, MULT)
+        def make_gate(t, cols):
+            entries = lists["n4"][:, cols.start // GROUP : cols.stop // GROUP]
+            nc.scalar.activation(gate[:, t, cols], y_or_st[t][:].indirect(entries), SIGMOID)
+
+        def finish(t, cols):
+            nc.vector.tensor_tensor(result[:, t, cols], h_plain[:, t, cols], gate[:, t, cols], MULT)
             nc.sync.dma_start(out_rows[:, t, cols], result[:, t, cols])
 
-        for t in range(last):
-            difference(t)
-            if t == 0:
-                for later in range(1, PACK):
-                    nc.vector.tensor_copy(h[:, later, halves[0]], second[later][:, halves[0]])
-            nc.scalar.activation(gate[:, t, :], first[t][:].indirect(lists["n4"][:]), SIGMOID)
-        difference(last)
+        whole = slice(0, S)
+        make_st(0)
+        for t in range(1, PACK):
+            nc.vector.tensor_copy(h_plain[:, t, halves[0]], d_or_h[t][:, halves[0]])
+        make_gate(0, whole)
+        nc.vector.tensor_copy(h_plain[:, 1, halves[1]], d_or_h[1][:, halves[1]])
+        for t in range(1, last):
+            make_st(t)
+            make_gate(t, whole)
+        make_st(last)
         for cols in halves:
-            entries = lists["n4"][:, cols.start // 16 : cols.stop // 16]
-            nc.scalar.activation(gate[:, last, cols], first[last][:].indirect(entries), SIGMOID)
+            make_gate(last, cols)
         for t in range(last):
-            finish(t, slice(0, S), gate[:, t, :])
+            finish(t, whole)
 
         rounded = sbuf("rounded", [P, PACK * S], BF16)
         out_words = sbuf("out_words", [P, S], I32)
         out_scales = sbuf("out_scales", [P, S], U8)
-        finish(last, halves[0], gate[:, last, halves[0]])
-        nc.vector.tensor_copy(woven(rounded, halves[0]), by_rows(result, halves[0]))
-        finish(last, halves[1], gate[:, last, halves[1]])
-        nc.scalar.copy(woven(rounded, slice(256, 384)), by_rows(result, slice(256, 384)))
-        nc.vector.tensor_copy(woven(rounded, slice(384, 512)), by_rows(result, slice(384, 512)))
+        finish(last, halves[0])
+        nc.vector.tensor_copy(woven(rounded, halves[0]), by_runs(result, halves[0]))
+        finish(last, halves[1])
+        nc.scalar.copy(woven(rounded, quarters[0]), by_runs(result, quarters[0]))
+        nc.vector.tensor_copy(woven(rounded, quarters[1]), by_runs(result, quarters[1]))
         for cols in halves:
-            nc.vector.quantize_mx(
-                out=out_words[:, cols].bitcast(FP8X4),
-                scales=out_scales[:, cols],
-                in_=rounded[:, PACK * cols.start : PACK * cols.stop],
-            )
+            quantise(nc, out_words, out_scales, rounded, cols)
             nc.sync.dma_start(words_in_hbm(out_1)[:, cols], out_words[:, cols])
         for q in range(QUADRANTS):
             queue = nc.scalar if q % 2 else nc.sync
-            queue.dma_start(out_2[0, 4 * q : 4 * q + 4, :].bitcast(I32), out_scales[32 * q : 32 * q + 4, :].bitcast(I32))
+            queue.dma_start(scale_rows_in_hbm(out_2, q), out_scales[scale_partitions(q, 0), :].bitcast(I32))

from contextlib import ExitStack

import concourse.mybir as mybir

K, T, S, H, N = 512, 2048, 512, 512, 512
FLOPS = 2 * S * (2 * K * H + H * N)

F32 = mybir.dt.float32
BF16 = mybir.dt.bfloat16
I32 = mybir.dt.int32
U32 = mybir.dt.uint32
U16 = mybir.dt.uint16
U8 = mybir.dt.uint8
FP8X4 = mybir.dt.float8_e4m3fn_x4
MULT = mybir.AluOpType.mult
SUBTRACT = mybir.AluOpType.subtract
COPY = mybir.ActivationFunctionType.Copy
SIGMOID = mybir.ActivationFunctionType.Sigmoid

P = 128
PACK = 4
QUADRANT = 32
QUADRANTS = P // QUADRANT
SCALE_ROWS = 4
GROUP = 16
BANKS = 8
HALF = S // 2
WINDOW = 2 * S
WORD_RUN, BYTE_RUN = 4, 16


def words_in_hbm(words):
    return words[0].rearrange("p n t -> p (n t)").bitcast(I32)


def scale_partitions(q, first):
    return slice(QUADRANT * q + first, QUADRANT * q + first + SCALE_ROWS)


def scale_rows_in_hbm(scales, q):
    return scales[0, SCALE_ROWS * q : SCALE_ROWS * (q + 1), :].bitcast(I32)


def load_scale_rows(queues, plane, first, scales):
    for q, queue in enumerate(queues):
        queue.dma_start(plane[scale_partitions(q, first), :].bitcast(I32), scale_rows_in_hbm(scales, q))


def deal_columns(nc, dealt, plain, run):
    nc.vector.tensor_copy(
        dealt[:].rearrange("p (t b i) -> p b t i", t=PACK, i=run),
        plain[:].rearrange("p (b i t) -> p b t i", t=PACK, i=run),
    )


def by_runs(tiles, cols):
    return tiles[:, :, cols].rearrange("p t (c i) -> p c t i", i=WORD_RUN)


def woven(tile, cols):
    return tile[:, PACK * cols.start : PACK * cols.stop].rearrange("p (c i t) -> p c t i", i=WORD_RUN, t=PACK)


def quantise(nc, words, scales, values, cols):
    nc.vector.quantize_mx(
        out=words[:, cols].bitcast(FP8X4),
        scales=scales[:, cols],
        in_=values[:, PACK * cols.start : PACK * cols.stop],
    )


def product(nc, out, weights, plane, t, codes, scales):
    nc.tensor.matmul_mx(
        out=out,
        lhsT=weights.bitcast(FP8X4),
        lhsT_scale=plane[:, P * t : P * (t + 1)],
        rhs=codes.bitcast(FP8X4),
        rhs_scale=scales,
        start=True,
        stop=True,
    )


def tile_picked_twlcrossbhopd_none_po_kernel(
    tc, x_words, x_scales, w1_words, w1_scales, w2_words, w2_scales, gn, w3_words, w3_scales,
    offs, two, n1, n2, n3, n4, out_0, out_1, out_2,
):
    nc = tc.nc
    halves = [slice(0, HALF), slice(HALF, S)]
    last = PACK - 1

    with ExitStack() as ctx:
        keep = ctx.enter_context(tc.tile_pool(name="keep", bufs=1))
        psum = ctx.enter_context(tc.psum_pool(name="psum", bufs=1))

        def sbuf(name, shape, dtype, slot=""):
            return keep.tile(shape, dtype, name=name, tag=slot, align_bytes=64)

        def bank(index, width):
            return psum.tile([P, width], F32, name="bank%d" % index)

        lists = {name: sbuf("list_" + name, [P, S // GROUP], U16) for name in ("offs", "two", "n1", "n2", "n3", "n4")}
        xw = sbuf("xw", [P, T], I32, slot="x_words_slot")
        xs = sbuf("xs", [P, T], U8)
        w12_plain = sbuf("w12_plain", [P, 2, H], I32)
        w12_first = sbuf("w12_first", [P, 2, P], I32)
        w3_plain = sbuf("w3_plain", [P, N], I32, slot="w3_words_slot")
        w3_dealt = sbuf("w3_dealt", [P, N], I32)
        s3_dealt = sbuf("s3_dealt", [P, N], U8)
        s12_plain = sbuf("s12_plain", [P, H], U8, slot="w12_scales_slot")
        s12_dealt = sbuf("s12_dealt", [P, H], U8)
        s3_plain = sbuf("s3_plain", [P, N], U8, slot="w3_scales_slot")
        gain_in = sbuf("gain_in", [P, PACK], F32)
        gain = sbuf("gain", [P, PACK], F32)
        y_or_st = [sbuf("y_or_st%d" % t, [P, WINDOW], F32) for t in range(PACK)]
        d_or_h = [sbuf("d_or_h%d" % t, [P, WINDOW], F32) for t in range(PACK)]

        warm = sbuf("warm", [P, 2], F32)
        nc.gpsimd.memset(xs[:].bitcast(I32), 0)
        nc.vector.memset(s12_plain[:].bitcast(I32), 0)
        nc.vector.memset(warm[:, 0:1], 0.0)
        nc.vector.memset(s3_plain[:].bitcast(I32), 0)
        nc.scalar.activation(warm[:, 1:2], warm[:, 0:1], SIGMOID)

        nc.sync.dma_start(lists["offs"][:], offs)
        nc.sync.dma_start(lists["two"][:], two)
        load_scale_rows([nc.sync] * QUADRANTS, xs, 0, x_scales)
        nc.sync.dma_start(xw[:], words_in_hbm(x_words))
        nc.sync.dma_start(w12_plain[:, 0, :], words_in_hbm(w1_words))
        nc.sync.dma_start(w12_plain[:, 1, :], words_in_hbm(w2_words))
        load_scale_rows([nc.sync] * QUADRANTS, s12_plain, 0, w1_scales)
        load_scale_rows([nc.gpsimd, nc.gpsimd, nc.gpsimd, nc.sync], s12_plain, SCALE_ROWS, w2_scales)
        nc.sync.dma_start(gain_in[:], gn.rearrange("(p t) o -> p (t o)", t=PACK))
        nc.sync.dma_start(lists["n2"][:], n2)
        nc.sync.dma_start(lists["n1"][:], n1)
        load_scale_rows([nc.sync] * QUADRANTS, s3_plain, 0, w3_scales)
        nc.sync.dma_start(w3_plain[:], words_in_hbm(w3_words))
        nc.sync.dma_start(lists["n3"][:], n3)
        nc.sync.dma_start(lists["n4"][:], n4)
        nc.scalar.mul(gain[:], gain_in[:], 0.75)

        words_offs = sbuf("words_offs", [P, S], U32)
        scales_offs = sbuf("scales_offs", [P, S], U8)
        scales_two = sbuf("scales_two", [P, S], U8)
        nc.vector.tensor_copy(scales_offs[:], xs[:].indirect(lists["offs"][:]))
        nc.vector.tensor_copy(scales_two[:], xs[:].indirect(lists["two"][:]))
        nc.vector.tensor_copy(words_offs[:], xw[:].bitcast(U32).indirect(lists["offs"][:]))
        w12_by_tile = w12_plain[:].rearrange("p w (b i t) -> p w b t i", t=PACK, i=WORD_RUN)
        nc.vector.tensor_copy(w12_first[:].rearrange("p w (b i) -> p w b i", i=WORD_RUN), w12_by_tile[:, :, :, 0, :])
        deal_columns(nc, s12_dealt, s12_plain, BYTE_RUN)
        words_two = sbuf("words_two", [P, S], U32, slot="w12_scales_slot")
        nc.vector.tensor_copy(words_two[:], xw[:].bitcast(U32).indirect(lists["two"][:]))
        w12_rest = sbuf("w12_rest", [P, 2, last, P], I32, slot="x_words_slot")
        nc.vector.tensor_copy(
            w12_rest[:].rearrange("p w t (b i) -> p w b t i", i=WORD_RUN), w12_by_tile[:, :, :, 1:, :]
        )

        for t in range(PACK):
            w12_tile = w12_rest[:, :, t - 1, :] if t else w12_first[:]
            acc = bank(t, S)
            product(nc, acc[:], w12_tile[:, 0, :], s12_dealt[0:P, :], t, words_offs[:], scales_offs[:])
            nc.scalar.activation(y_or_st[t][:, :S], acc[:], COPY, scale=gain[:, t : t + 1])
            acc = bank(PACK + t, S)
            product(nc, acc[:], w12_tile[:, 1, :], s12_dealt[SCALE_ROWS:P, :], t, words_two[:], scales_two[:])
            nc.scalar.copy(d_or_h[t][:, :S], acc[:])

        deal_columns(nc, s3_dealt, s3_plain, BYTE_RUN)
        deal_columns(nc, w3_dealt, w3_plain, WORD_RUN)

        plus = sbuf("plus", [P, PACK, S], F32, slot="w3_words_slot")
        minus = sbuf("minus", [P, PACK, S], F32, slot="w3_scales_slot")
        for t in range(PACK):
            nc.vector.tensor_tensor(plus[:, t, :], d_or_h[t][:].indirect(lists["n2"][:]), y_or_st[t][:, :S], MULT)
            nc.vector.tensor_tensor(minus[:, t, :], y_or_st[t][:].indirect(lists["n1"][:]), d_or_h[t][:, :S], MULT)

        z = sbuf("z", [P, PACK * S], BF16)
        z_words = sbuf("z_words", [P, S], U32)
        z_scales = sbuf("z_scales", [P, S], U8)
        quarters = [slice(HALF, HALF + S // 4), slice(HALF + S // 4, S)]
        pieces = [halves[0]] + quarters
        for c, cols in enumerate(pieces):
            nc.vector.tensor_tensor(woven(z, cols), by_runs(plus, cols), by_runs(minus, cols), SUBTRACT)
            if c:
                quantise(nc, z_words, z_scales, z, pieces[c - 1])
        quantise(nc, z_words, z_scales, z, pieces[-1])

        h_plain = sbuf("h_plain", [P, PACK, S], F32)
        for c, cols in enumerate(pieces):
            acc = bank(PACK + c, cols.stop - cols.start)
            product(nc, acc[:], w3_dealt[:, :P], s3_dealt[:], 0, z_words[:, cols], z_scales[:, cols])
            nc.scalar.copy(d_or_h[0][:, cols], acc[:])
            nc.vector.tensor_copy(h_plain[:, 0, cols], d_or_h[0][:, cols])
        next_bank = PACK + len(pieces)
        for c, cols in enumerate(halves):
            for t in range(1, PACK):
                acc = bank((next_bank + last * c + t - 1) % BANKS, HALF)
                product(
                    nc, acc[:], w3_dealt[:, P * t : P * (t + 1)], s3_dealt[:], t, z_words[:, cols], z_scales[:, cols]
                )
                nc.scalar.copy(d_or_h[t][:, cols], acc[:])
        for t in range(2, PACK):
            nc.scalar.copy(h_plain[:, t, halves[1]], d_or_h[t][:, halves[1]])

        gate = sbuf("gate", [P, PACK, S], F32)
        result = sbuf("result", [P, PACK, S], F32)
        out_rows = out_0.rearrange("(p t) s -> p t s", t=PACK)

        def make_st(t):
            nc.vector.tensor_tensor(
                y_or_st[t][:, :S], d_or_h[t][:].indirect(lists["n3"][:]), h_plain[:, t, :], SUBTRACT
            )

        def make_gate(t, cols):
            entries = lists["n4"][:, cols.start // GROUP : cols.stop // GROUP]
            nc.scalar.activation(gate[:, t, cols], y_or_st[t][:].indirect(entries), SIGMOID)

        def finish(t, cols):
            nc.vector.tensor_tensor(result[:, t, cols], h_plain[:, t, cols], gate[:, t, cols], MULT)
            nc.sync.dma_start(out_rows[:, t, cols], result[:, t, cols])

        whole = slice(0, S)
        make_st(0)
        for t in range(1, PACK):
            nc.vector.tensor_copy(h_plain[:, t, halves[0]], d_or_h[t][:, halves[0]])
        make_gate(0, whole)
        nc.vector.tensor_copy(h_plain[:, 1, halves[1]], d_or_h[1][:, halves[1]])
        for t in range(1, last):
            make_st(t)
            make_gate(t, whole)
        make_st(last)
        for cols in halves:
            make_gate(last, cols)
        for t in range(last):
            finish(t, whole)

        rounded = sbuf("rounded", [P, PACK * S], BF16)
        out_words = sbuf("out_words", [P, S], I32)
        out_scales = sbuf("out_scales", [P, S], U8)
        finish(last, halves[0])
        nc.vector.tensor_copy(woven(rounded, halves[0]), by_runs(result, halves[0]))
        finish(last, halves[1])
        nc.scalar.copy(woven(rounded, quarters[0]), by_runs(result, quarters[0]))
        nc.vector.tensor_copy(woven(rounded, quarters[1]), by_runs(result, quarters[1]))
        for cols in halves:
            quantise(nc, out_words, out_scales, rounded, cols)
            nc.sync.dma_start(words_in_hbm(out_1)[:, cols], out_words[:, cols])
        for q in range(QUADRANTS):
            queue = nc.scalar if q % 2 else nc.sync
            queue.dma_start(scale_rows_in_hbm(out_2, q), out_scales[scale_partitions(q, 0), :].bitcast(I32))
